import numpy as np
CORES = [23,119,17,113]
N = 4
S, B = 4, 64
def setup_inputs(rng):
    a = (rng.standard_normal((128, 128), dtype=np.float32) / 12)
    return {"x": rng.standard_normal((N, 128, S * B), dtype=np.float32), "a": np.broadcast_to(a, (N, 128, 128)).copy(), "at": np.broadcast_to(a.T, (N, 128, 128)).copy()}
def setup_inputs_big(rng):
    d = setup_inputs(rng)
    for k in ("x",): d[k] = (d[k].astype(np.float32) * 1048576.0).astype(d[k].dtype)
    return d
def setup_inputs_small(rng):
    d = setup_inputs(rng)
    for k in ("x",): d[k] = (d[k].astype(np.float32) * (1 / 1048576.0)).astype(d[k].dtype)
    return d
def setup_inputs_apart(rng):
    d = setup_inputs(rng)
    f = (10.0 ** rng.permutation(np.linspace(-1.5, 1.5, N))).astype(np.float32).reshape(N, 1, 1)
    for k in ("x",): d[k] = (d[k].astype(np.float32) * f).astype(d[k].dtype)
    return d
def reference(x, a, at):
    X, A = x.astype(np.float64), a.astype(np.float64)
    y = np.zeros((N, 128, S * B)); h = np.zeros((128, B))
    for r in range(N):
        for s in range(S):
            h = A[r].T @ h + X[r][:, B * s:B * s + B]
            y[r][:, B * s:B * s + B] = h
    return {"y": y.astype(np.float32)}

@@ -1,0 +1,193 @@
+from concourse.bass import DstId, RemoteDMATransfer
+from concourse.mybir import AluOpType
+
+B = 64
+S = 4
+E_FAR = 4
+E_NEAR = 4
+N_EVENTS = 40
+
+SCRATCH = {
+    "xs": ("sbuf", [128, S * B], "float32"),
+    "ls": ("sbuf", [128, S * B], "float32"),
+    "ys": ("sbuf", [128, S * B], "float32"),
+    "pw": ("sbuf", [128, 4 * 128], "float32"),
+    "ats": ("sbuf", [128, 128], "float32"),
+    "at2": ("sbuf", [128, 128], "float32"),
+    "at4": ("sbuf", [128, 128], "float32"),
+    "p8": ("sbuf", [128, 128], "float32"),
+    "land0": ("sbuf", [128, B], "float32"),
+    "land1": ("sbuf", [128, B], "float32"),
+    "land2": ("sbuf", [128, B], "float32"),
+    "hs": ("sbuf", [128, B], "float32"),
+    "psh": ("psum", [128, 512], "float32"),
+    "psa": ("psum", [128, 512], "float32"),
+    "psb": ("psum", [128, 512], "float32"),
+    "psc": ("psum", [128, 512], "float32"),
+    "psg": ("psum", [128, 512], "float32"),
+}
+SEMAPHORES = ["arr0", "arr1", "arr2", "sent"] + ["e%d" % i for i in range(N_EVENTS)]
+
+
+def _engines(mask):
+    return [i for i in range(mask.bit_length()) if (mask >> i) & 1]
+
+
+def _thin(pool, n):
+    n = min(n, len(pool))
+    return pool[::len(pool) // n][:n]
+
+
+def _plan(core, dests, topo):
+    far = [d for d in dests if topo.chip(d) != topo.chip(core)]
+    near = [d for d in dests if topo.chip(d) == topo.chip(core)]
+    far_pool = _engines(topo.mask(core, far[0])) if far else []
+    plan = {}
+    for j, d in enumerate(far):
+        plan[d] = _thin(far_pool[j::len(far)], E_FAR)
+    for j, d in enumerate(near):
+        pool = [e for e in _engines(topo.mask(core, d)) if e not in far_pool]
+        plan[d] = _thin(pool[j::len(near)], E_NEAR)
+    return plan
+
+
+def rank_program(g, core, T, topo):
+    r = T.rank_of(core)
+    if r is None:
+        return
+    n = len(T.cores)
+    te, ve, sy, sc = g.tensor, g.vector, g.sync, g.scalar
+    add = AluOpType.add
+    used = [0]
+
+    def ev():
+        used[0] += 1
+        return T.sem["e%d" % (used[0] - 1)]
+
+    def col(t, s, w=B):
+        return t[:, s * w:(s + 1) * w]
+
+    def power(k):
+        return col(T.pw, k - 1, 128)
+
+    a = power(1)
+    last = r == n - 1
+    plans = [_plan(c, T.cores[q + 1:], topo) for q, c in enumerate(T.cores)]
+    arrives = [len(plans[q][core]) for q in range(r)]
+
+    s_x, s_a, s_at = ev(), ev(), ev()
+    sc.dma_start(a, T.a[:]).then_inc(s_a, 16)
+    if last:
+        sy.dma_start(T.ats[:], T.at[:]).then_inc(s_at, 16)
+        sy.dma_start(T.xs[:], T.x[:]).then_inc(s_x, 16)
+    else:
+        sy.dma_start(T.xs[:], T.x[:]).then_inc(s_x, 16)
+        if r > 0:
+            sc.dma_start(T.ats[:], T.at[:]).then_inc(s_at, 16)
+
+    s_l = [ev() for _ in range(S)]
+
+    def scan_first():
+        ve.wait_ge(s_x, 16)
+        ve.tensor_copy(col(T.ls, 0), col(T.xs, 0)).then_inc(s_l[0], 1)
+        te.wait_ge(s_x, 16)
+
+    def scan_step(s):
+        m = ev()
+        if s > 1:
+            te.wait_ge(s_l[s - 1], 1)
+        te.matmul(T.psh[:, 0:B], a, col(T.xs, 0) if s == 1 else col(T.ls, s - 1), True, True).then_inc(m, 1)
+        ve.wait_ge(m, 1)
+        ve.tensor_tensor(col(T.ls, s), T.psh[:, 0:B], col(T.xs, s), add).then_inc(s_l[s], 1)
+
+    def product(bank, lhsT, rhs, out, w=128):
+        m, c = ev(), ev()
+        te.matmul(bank[:, 0:w], lhsT, rhs, True, True).then_inc(m, 1)
+        return (m, c, bank[:, 0:w], out)
+
+    def fetch(p):
+        m, c, src, out = p
+        ve.wait_ge(m, 1)
+        ve.tensor_copy(out, src).then_inc(c, 1)
+        return c
+
+    te.wait_ge(s_a, 16)
+    if not last:
+        scan_first()
+        for s in range(1, S):
+            scan_step(s)
+        if r > 0:
+            te.wait_ge(s_at, 16)
+            for k, bank in ((2, T.psa), (3, T.psb), (4, T.psc)):
+                te.wait_ge(fetch(product(bank, T.ats[:], power(k - 1), power(k))), 1)
+    else:
+        te.wait_ge(s_at, 16)
+        p2 = product(T.psa, T.ats[:], a, power(2))
+        t2 = product(T.psb, a, T.ats[:], T.at2[:])
+        c2, ct2 = fetch(p2), fetch(t2)
+        scan_first()
+        scan_step(1)
+        te.wait_ge(c2, 1)
+        te.wait_ge(ct2, 1)
+        p34 = product(T.psc, T.at2[:], T.pw[:, 0:256], T.pw[:, 256:512], 256)
+        t4 = product(T.psa, power(2), T.at2[:], T.at4[:])
+        c34, ct4 = fetch(p34), fetch(t4)
+        scan_step(2)
+        te.wait_ge(c34, 1)
+        te.wait_ge(ct4, 1)
+        p8 = product(T.psb, T.at4[:], power(4), T.p8[:])
+        c8 = fetch(p8)
+        scan_step(3)
+        te.wait_ge(c8, 1)
+
+    if not last:
+        src = col(T.ls, S - 1)
+        land, arr = T["land%d" % r], T.sem["arr%d" % r]
+        plan = plans[r]
+        transfers = []
+        for d in T.cores[r + 1:]:
+            rid, pid, _ = topo.addr(d)
+            transfers.append(RemoteDMATransfer(dst_ids=[DstId(rid=rid, pnc=pid)],
+                                               dma_engine_mask=sum(1 << e for e in plan[d]),
+                                               remote_sem=arr, src=src, dst=land[:]))
+        g.wait_ge(s_l[S - 1], 1)
+        g.remote_dma_fused(transfers, local_sem=T.sem.sent)
+        g.wait_ge(T.sem.sent, sum(len(plan[d]) for d in plan))
+
+    s_st = ev()
+    if r == 0:
+        for s in range(S):
+            sy.wait_ge(s_l[s], 1)
+        sy.dma_start(T.y[:], T.ls[:]).then_inc(s_st, 16)
+        sy.wait_ge(s_st, 16)
+        return
+
+    te.wait_ge(s_l[S - 1], 1)
+    for s in range(S):
+        ve.wait_ge(s_l[s], 1)
+    if r == 1:
+        te.wait_ge(T.sem.arr0, arrives[0])
+        h = T.land0[:]
+    else:
+        early = sorted(range(r - 1), key=lambda q: topo.chip(T.cores[q]) != topo.chip(core))
+        m, s_h = ev(), ev()
+        for i, q in enumerate(early):
+            te.wait_ge(T.sem["arr%d" % q], arrives[q])
+            mat = power(4) if r - 1 - q == 1 else T.p8[:]
+            ins = te.matmul(T.psg[:, 0:B], mat, T["land%d" % q][:], i == 0, i == len(early) - 1)
+        ins.then_inc(m, 1)
+        ve.wait_ge(T.sem["arr%d" % (r - 1)], arrives[r - 1])
+        ve.wait_ge(m, 1)
+        ve.tensor_tensor(T.hs[:], T.psg[:, 0:B], T["land%d" % (r - 1)][:], add).then_inc(s_h, 1)
+        te.wait_ge(s_h, 1)
+        h = T.hs[:]
+
+    s_y = ev()
+    for s, bank in enumerate((T.psa, T.psb, T.psc, T.psh)):
+        m = ev()
+        te.matmul(bank[:, 0:B], power(s + 1), h, True, True).then_inc(m, 1)
+        ve.wait_ge(m, 1)
+        ve.tensor_tensor(col(T.ys, s), bank[:, 0:B], col(T.ls, s), add).then_inc(s_y, 1)
+    sy.wait_ge(s_y, S)
+    sy.dma_start(T.y[:], T.ys[:]).then_inc(s_st, 16)
+    sy.wait_ge(s_st, 16)

@@ -3,22 +3,28 @@ from concourse.mybir import AluOpType
 
 B = 64
 S = 4
-E_FAR = 4
-E_NEAR = 4
 N_EVENTS = 40
 
 SCRATCH = {
     "xs": ("sbuf", [128, S * B], "float32"),
     "ls": ("sbuf", [128, S * B], "float32"),
     "ys": ("sbuf", [128, S * B], "float32"),
-    "pw": ("sbuf", [128, 4 * 128], "float32"),
+    "cs": ("sbuf", [128, 2 * B], "float32"),
+    "p1": ("sbuf", [128, 128], "float32"),
+    "p2": ("sbuf", [128, 128], "float32"),
+    "p4": ("sbuf", [128, 128], "float32"),
+    "p8": ("sbuf", [128, 128], "float32"),
     "ats": ("sbuf", [128, 128], "float32"),
     "at2": ("sbuf", [128, 128], "float32"),
     "at4": ("sbuf", [128, 128], "float32"),
-    "p8": ("sbuf", [128, 128], "float32"),
     "land0": ("sbuf", [128, B], "float32"),
     "land1": ("sbuf", [128, B], "float32"),
     "land2": ("sbuf", [128, B], "float32"),
+    "lx0": ("sbuf", [128, B], "float32"),
+    "lx1": ("sbuf", [128, B], "float32"),
+    "lx2": ("sbuf", [128, B], "float32"),
+    "zs": ("sbuf", [128, B], "float32"),
+    "ts": ("sbuf", [128, B], "float32"),
     "hs": ("sbuf", [128, B], "float32"),
     "psh": ("psum", [128, 512], "float32"),
     "psa": ("psum", [128, 512], "float32"),
@@ -26,29 +32,22 @@ SCRATCH = {
     "psc": ("psum", [128, 512], "float32"),
     "psg": ("psum", [128, 512], "float32"),
 }
-SEMAPHORES = ["arr0", "arr1", "arr2", "sent"] + ["e%d" % i for i in range(N_EVENTS)]
+SEMAPHORES = ["arr0", "arr1", "arr2", "arx0", "arx1", "arx2", "sent"] + ["e%d" % i for i in range(N_EVENTS)]
 
 
 def _engines(mask):
     return [i for i in range(mask.bit_length()) if (mask >> i) & 1]
 
 
-def _thin(pool, n):
-    n = min(n, len(pool))
-    return pool[::len(pool) // n][:n]
-
-
 def _plan(core, dests, topo):
-    far = [d for d in dests if topo.chip(d) != topo.chip(core)]
+    far = [d for d in reversed(dests) if topo.chip(d) != topo.chip(core)]
     near = [d for d in dests if topo.chip(d) == topo.chip(core)]
     far_pool = _engines(topo.mask(core, far[0])) if far else []
-    plan = {}
-    for j, d in enumerate(far):
-        plan[d] = _thin(far_pool[j::len(far)], E_FAR)
+    calls = [[(d, far_pool)] for d in far] or [[]]
     for j, d in enumerate(near):
         pool = [e for e in _engines(topo.mask(core, d)) if e not in far_pool]
-        plan[d] = _thin(pool[j::len(near)], E_NEAR)
-    return plan
+        calls[0].append((d, pool[j::len(near)]))
+    return calls
 
 
 def rank_program(g, core, T, topo):
@@ -64,130 +63,147 @@ def rank_program(g, core, T, topo):
         used[0] += 1
         return T.sem["e%d" % (used[0] - 1)]
 
-    def col(t, s, w=B):
-        return t[:, s * w:(s + 1) * w]
+    def col(t, s):
+        return t[:, s * B:(s + 1) * B]
 
-    def power(k):
-        return col(T.pw, k - 1, 128)
+    def l(s):
+        return col(T.xs, 0) if s == 0 else col(T.ls, s)
 
-    a = power(1)
+    a, p2, p4, p8, at, at2, at4 = T.p1[:], T.p2[:], T.p4[:], T.p8[:], T.ats[:], T.at2[:], T.at4[:]
     last = r == n - 1
-    plans = [_plan(c, T.cores[q + 1:], topo) for q, c in enumerate(T.cores)]
-    arrives = [len(plans[q][core]) for q in range(r)]
+    plans = [_plan(c, T.cores[q + 1:], topo) for q, c in enumerate(T.cores[:-1])]
+    arrives = [sum(len(e) for call in plans[q] for d, e in call if d == core) for q in range(r)]
 
     s_x, s_a, s_at = ev(), ev(), ev()
     sc.dma_start(a, T.a[:]).then_inc(s_a, 16)
     if last:
-        sy.dma_start(T.ats[:], T.at[:]).then_inc(s_at, 16)
+        sy.dma_start(at, T.at[:]).then_inc(s_at, 16)
         sy.dma_start(T.xs[:], T.x[:]).then_inc(s_x, 16)
     else:
         sy.dma_start(T.xs[:], T.x[:]).then_inc(s_x, 16)
         if r > 0:
-            sc.dma_start(T.ats[:], T.at[:]).then_inc(s_at, 16)
+            sc.dma_start(at, T.at[:]).then_inc(s_at, 16)
 
-    s_l = [ev() for _ in range(S)]
-
-    def scan_first():
-        ve.wait_ge(s_x, 16)
-        ve.tensor_copy(col(T.ls, 0), col(T.xs, 0)).then_inc(s_l[0], 1)
-        te.wait_ge(s_x, 16)
+    s_l = [None] + [ev() for _ in range(1, S)]
+    s_z = ev()
 
     def scan_step(s):
         m = ev()
-        if s > 1:
+        if s == 1:
+            te.wait_ge(s_x, 16)
+            ve.wait_ge(s_x, 16)
+        else:
             te.wait_ge(s_l[s - 1], 1)
-        te.matmul(T.psh[:, 0:B], a, col(T.xs, 0) if s == 1 else col(T.ls, s - 1), True, True).then_inc(m, 1)
+        te.matmul(T.psh[:, 0:B], a, l(s - 1), True, True).then_inc(m, 1)
         ve.wait_ge(m, 1)
-        ve.tensor_tensor(col(T.ls, s), T.psh[:, 0:B], col(T.xs, s), add).then_inc(s_l[s], 1)
+        if s == S - 1 and not last:
+            ve.tensor_copy(T.zs[:], T.psh[:, 0:B]).then_inc(s_z, 1)
+        ve.tensor_tensor(l(s), T.psh[:, 0:B], col(T.xs, s), add).then_inc(s_l[s], 1)
 
-    def product(bank, lhsT, rhs, out, w=128):
-        m, c = ev(), ev()
-        te.matmul(bank[:, 0:w], lhsT, rhs, True, True).then_inc(m, 1)
-        return (m, c, bank[:, 0:w], out)
+    def products(*todo):
+        done = []
+        for bank, lhsT, rhs, out in todo:
+            m = ev()
+            te.matmul(bank[:, 0:128], lhsT, rhs, True, True).then_inc(m, 1)
+            done.append(m)
+        sems = []
+        for (bank, lhsT, rhs, out), m in zip(todo, done):
+            c = ev()
+            ve.wait_ge(m, 1)
+            ve.tensor_copy(out, bank[:, 0:128]).then_inc(c, 1)
+            sems.append(c)
+        return sems
 
-    def fetch(p):
-        m, c, src, out = p
-        ve.wait_ge(m, 1)
-        ve.tensor_copy(out, src).then_inc(c, 1)
-        return c
+    def te_wait(sems):
+        for c in sems:
+            te.wait_ge(c, 1)
 
     te.wait_ge(s_a, 16)
     if not last:
-        scan_first()
         for s in range(1, S):
             scan_step(s)
-        if r > 0:
+        if r == 1:
             te.wait_ge(s_at, 16)
-            for k, bank in ((2, T.psa), (3, T.psb), (4, T.psc)):
-                te.wait_ge(fetch(product(bank, T.ats[:], power(k - 1), power(k))), 1)
+            te_wait(products((T.psa, at, a, p2)))
+        if r > 1:
+            te.wait_ge(s_at, 16)
+            te_wait(products((T.psa, at, a, p2), (T.psb, a, at, at2)))
+            te_wait(products((T.psc, at2, p2, p4)))
     else:
         te.wait_ge(s_at, 16)
-        p2 = product(T.psa, T.ats[:], a, power(2))
-        t2 = product(T.psb, a, T.ats[:], T.at2[:])
-        c2, ct2 = fetch(p2), fetch(t2)
-        scan_first()
+        c = products((T.psa, at, a, p2), (T.psb, a, at, at2))
         scan_step(1)
-        te.wait_ge(c2, 1)
-        te.wait_ge(ct2, 1)
-        p34 = product(T.psc, T.at2[:], T.pw[:, 0:256], T.pw[:, 256:512], 256)
-        t4 = product(T.psa, power(2), T.at2[:], T.at4[:])
-        c34, ct4 = fetch(p34), fetch(t4)
+        te_wait(c)
+        c = products((T.psc, at2, p2, p4), (T.psa, p2, at2, at4))
         scan_step(2)
-        te.wait_ge(c34, 1)
-        te.wait_ge(ct4, 1)
-        p8 = product(T.psb, T.at4[:], power(4), T.p8[:])
-        c8 = fetch(p8)
+        te_wait(c)
+        c = products((T.psb, at4, p4, p8))
         scan_step(3)
-        te.wait_ge(c8, 1)
+        te_wait(c)
 
     if not last:
-        src = col(T.ls, S - 1)
-        land, arr = T["land%d" % r], T.sem["arr%d" % r]
-        plan = plans[r]
-        transfers = []
-        for d in T.cores[r + 1:]:
-            rid, pid, _ = topo.addr(d)
-            transfers.append(RemoteDMATransfer(dst_ids=[DstId(rid=rid, pnc=pid)],
-                                               dma_engine_mask=sum(1 << e for e in plan[d]),
-                                               remote_sem=arr, src=src, dst=land[:]))
-        g.wait_ge(s_l[S - 1], 1)
-        g.remote_dma_fused(transfers, local_sem=T.sem.sent)
-        g.wait_ge(T.sem.sent, sum(len(plan[d]) for d in plan))
+        total = 0
+        for sem, src, land, arr in ((s_x, col(T.xs, S - 1), "lx%d", "arx%d"), (s_z, T.zs[:], "land%d", "arr%d")):
+            g.wait_ge(sem, 16 if sem is s_x else 1)
+            for call in plans[r]:
+                transfers = []
+                for d, engines in call:
+                    rid, pid, _ = topo.addr(d)
+                    transfers.append(RemoteDMATransfer(dst_ids=[DstId(rid=rid, pnc=pid)],
+                                                       dma_engine_mask=sum(1 << e for e in engines),
+                                                       remote_sem=T.sem[arr % r], src=src, dst=T[land % r][:]))
+                    total += len(engines)
+                g.remote_dma_fused(transfers, local_sem=T.sem.sent)
+        g.wait_ge(T.sem.sent, total)
 
-    s_st = ev()
+    s_st0, s_st1 = ev(), ev()
     if r == 0:
-        for s in range(S):
+        sc.wait_ge(s_x, 16)
+        sc.dma_start(col(T.y, 0), l(0)).then_inc(s_st1, 16)
+        sc.wait_ge(s_st1, 16)
+        for s in range(1, S):
             sy.wait_ge(s_l[s], 1)
-        sy.dma_start(T.y[:], T.ls[:]).then_inc(s_st, 16)
-        sy.wait_ge(s_st, 16)
+        sy.dma_start(T.y[:, B:S * B], T.ls[:, B:S * B]).then_inc(s_st0, 16)
+        sy.wait_ge(s_st0, 16)
         return
 
     te.wait_ge(s_l[S - 1], 1)
-    for s in range(S):
+    for s in range(1, S):
         ve.wait_ge(s_l[s], 1)
-    if r == 1:
-        te.wait_ge(T.sem.arr0, arrives[0])
-        h = T.land0[:]
-    else:
-        early = sorted(range(r - 1), key=lambda q: topo.chip(T.cores[q]) != topo.chip(core))
-        m, s_h = ev(), ev()
-        for i, q in enumerate(early):
-            te.wait_ge(T.sem["arr%d" % q], arrives[q])
-            mat = power(4) if r - 1 - q == 1 else T.p8[:]
-            ins = te.matmul(T.psg[:, 0:B], mat, T["land%d" % q][:], i == 0, i == len(early) - 1)
+    s_t, s_h = ev(), ev()
+    p = r - 1
+    ve.wait_ge(T.sem["arx%d" % p], arrives[p])
+    ve.wait_ge(T.sem["arr%d" % p], arrives[p])
+    ve.tensor_tensor((T.hs if r == 1 else T.ts)[:], T["lx%d" % p][:], T["land%d" % p][:], add).then_inc(s_h if r == 1 else s_t, 1)
+    if r > 1:
+        early = sorted(range(p), key=lambda q: topo.chip(T.cores[q]) != topo.chip(core))
+        parts = [("lx%d", "arx%d", q) for q in early] + [("land%d", "arr%d", q) for q in early]
+        m = ev()
+        for i, (land, arr, q) in enumerate(parts):
+            te.wait_ge(T.sem[arr % q], arrives[q])
+            ins = te.matmul(T.psg[:, 0:B], p4 if p - q == 1 else p8, T[land % q][:], i == 0, i == len(parts) - 1)
         ins.then_inc(m, 1)
-        ve.wait_ge(T.sem["arr%d" % (r - 1)], arrives[r - 1])
+        ve.wait_ge(s_t, 1)
         ve.wait_ge(m, 1)
-        ve.tensor_tensor(T.hs[:], T.psg[:, 0:B], T["land%d" % (r - 1)][:], add).then_inc(s_h, 1)
-        te.wait_ge(s_h, 1)
-        h = T.hs[:]
+        ve.tensor_tensor(T.hs[:], T.psg[:, 0:B], T.ts[:], add).then_inc(s_h, 1)
+    te.wait_ge(s_h, 1)
+    h = T.hs[:]
 
-    s_y = ev()
+    s_c = [ev(), ev()]
+    s_y = [ev(), ev()]
     for s, bank in enumerate((T.psa, T.psb, T.psc, T.psh)):
         m = ev()
-        te.matmul(bank[:, 0:B], power(s + 1), h, True, True).then_inc(m, 1)
+        if s >= 2:
+            te.wait_ge(s_c[s - 2], 1)
+        te.matmul(bank[:, 0:B], a if s == 0 else p2, h if s < 2 else col(T.cs, s - 2), True, True).then_inc(m, 1)
         ve.wait_ge(m, 1)
-        ve.tensor_tensor(col(T.ys, s), bank[:, 0:B], col(T.ls, s), add).then_inc(s_y, 1)
-    sy.wait_ge(s_y, S)
-    sy.dma_start(T.y[:], T.ys[:]).then_inc(s_st, 16)
-    sy.wait_ge(s_st, 16)
+        if s < 2:
+            ve.tensor_copy(col(T.cs, s), bank[:, 0:B]).then_inc(s_c[s], 1)
+        ve.tensor_tensor(col(T.ys, s), bank[:, 0:B], l(s), add).then_inc(s_y[s // 2], 1)
+    half = S * B // 2
+    sy.wait_ge(s_y[0], 2)
+    sy.dma_start(T.y[:, 0:half], T.ys[:, 0:half]).then_inc(s_st0, 16)
+    sc.wait_ge(s_y[1], 2)
+    sc.dma_start(T.y[:, half:2 * half], T.ys[:, half:2 * half]).then_inc(s_st1, 16)
+    sy.wait_ge(s_st0, 16)
+    sc.wait_ge(s_st1, 16)

@@ -3,13 +3,12 @@ from concourse.mybir import AluOpType
 
 B = 64
 S = 4
-N_EVENTS = 40
+N_EVENTS = 48
 
 SCRATCH = {
     "xs": ("sbuf", [128, S * B], "float32"),
     "ls": ("sbuf", [128, S * B], "float32"),
     "ys": ("sbuf", [128, S * B], "float32"),
-    "cs": ("sbuf", [128, 2 * B], "float32"),
     "p1": ("sbuf", [128, 128], "float32"),
     "p2": ("sbuf", [128, 128], "float32"),
     "p4": ("sbuf", [128, 128], "float32"),
@@ -27,9 +26,12 @@ SCRATCH = {
     "ts": ("sbuf", [128, B], "float32"),
     "hs": ("sbuf", [128, B], "float32"),
     "psh": ("psum", [128, 512], "float32"),
+    "psz": ("psum", [128, 512], "float32"),
     "psa": ("psum", [128, 512], "float32"),
     "psb": ("psum", [128, 512], "float32"),
     "psc": ("psum", [128, 512], "float32"),
+    "pse": ("psum", [128, 512], "float32"),
+    "psf": ("psum", [128, 512], "float32"),
     "psg": ("psum", [128, 512], "float32"),
 }
 SEMAPHORES = ["arr0", "arr1", "arr2", "arx0", "arx1", "arx2", "sent"] + ["e%d" % i for i in range(N_EVENTS)]
@@ -66,10 +68,11 @@ def rank_program(g, core, T, topo):
     def col(t, s):
         return t[:, s * B:(s + 1) * B]
 
-    def l(s):
-        return col(T.xs, 0) if s == 0 else col(T.ls, s)
+    def x(s):
+        return col(T.xs, s)
 
     a, p2, p4, p8, at, at2, at4 = T.p1[:], T.p2[:], T.p4[:], T.p8[:], T.ats[:], T.at2[:], T.at4[:]
+    l1, l2, l3 = col(T.ls, 1), col(T.ls, 2), col(T.ls, 3)
     last = r == n - 1
     plans = [_plan(c, T.cores[q + 1:], topo) for q, c in enumerate(T.cores[:-1])]
     arrives = [sum(len(e) for call in plans[q] for d, e in call if d == core) for q in range(r)]
@@ -81,70 +84,58 @@ def rank_program(g, core, T, topo):
         sy.dma_start(T.xs[:], T.x[:]).then_inc(s_x, 16)
     else:
         sy.dma_start(T.xs[:], T.x[:]).then_inc(s_x, 16)
-        if r > 0:
-            sc.dma_start(at, T.at[:]).then_inc(s_at, 16)
+        sc.dma_start(at, T.at[:]).then_inc(s_at, 16)
 
-    s_l = [None] + [ev() for _ in range(1, S)]
-    s_z = ev()
-
-    def scan_step(s):
+    def mm(bank, lhsT, rhs, start=True, stop=True, w=B):
+        ins = te.matmul(bank[:, 0:w], lhsT, rhs, start, stop)
+        if not stop:
+            return None
         m = ev()
-        if s == 1:
-            te.wait_ge(s_x, 16)
-            ve.wait_ge(s_x, 16)
-        else:
-            te.wait_ge(s_l[s - 1], 1)
-        te.matmul(T.psh[:, 0:B], a, l(s - 1), True, True).then_inc(m, 1)
+        ins.then_inc(m, 1)
+        return m
+
+    def vcopy(out, bank, m, w=B):
         ve.wait_ge(m, 1)
-        if s == S - 1 and not last:
-            ve.tensor_copy(T.zs[:], T.psh[:, 0:B]).then_inc(s_z, 1)
-        ve.tensor_tensor(l(s), T.psh[:, 0:B], col(T.xs, s), add).then_inc(s_l[s], 1)
+        c = ev()
+        ve.tensor_copy(out, bank[:, 0:w]).then_inc(c, 1)
+        return c
 
-    def products(*todo):
-        done = []
-        for bank, lhsT, rhs, out in todo:
-            m = ev()
-            te.matmul(bank[:, 0:128], lhsT, rhs, True, True).then_inc(m, 1)
-            done.append(m)
-        sems = []
-        for (bank, lhsT, rhs, out), m in zip(todo, done):
-            c = ev()
-            ve.wait_ge(m, 1)
-            ve.tensor_copy(out, bank[:, 0:128]).then_inc(c, 1)
-            sems.append(c)
-        return sems
+    def pmm(bank, lhsT, rhs):
+        return mm(bank, lhsT, rhs, True, True, 128)
 
-    def te_wait(sems):
-        for c in sems:
-            te.wait_ge(c, 1)
+    def pcopy(out, bank, m):
+        return vcopy(out, bank, m, 128)
+
+    def vadd(out, in0, in1, *after):
+        for w in after:
+            ve.wait_ge(w, 1)
+        c = ev()
+        ve.tensor_tensor(out, in0, in1, add).then_inc(c, 1)
+        return c
+
+    def ps(bank):
+        return bank[:, 0:B]
+
+    def landed(queue, kind, q):
+        queue.wait_ge(T.sem[kind % q], arrives[q])
 
     te.wait_ge(s_a, 16)
+    ve.wait_ge(s_x, 16)
     if not last:
-        for s in range(1, S):
-            scan_step(s)
-        if r == 1:
-            te.wait_ge(s_at, 16)
-            te_wait(products((T.psa, at, a, p2)))
-        if r > 1:
-            te.wait_ge(s_at, 16)
-            te_wait(products((T.psa, at, a, p2), (T.psb, a, at, at2)))
-            te_wait(products((T.psc, at2, p2, p4)))
-    else:
+        te.wait_ge(s_x, 16)
+        s_l1 = vadd(l1, ps(T.psh), x(1), mm(T.psh, a, x(0)))
         te.wait_ge(s_at, 16)
-        c = products((T.psa, at, a, p2), (T.psb, a, at, at2))
-        scan_step(1)
-        te_wait(c)
-        c = products((T.psc, at2, p2, p4), (T.psa, p2, at2, at4))
-        scan_step(2)
-        te_wait(c)
-        c = products((T.psb, at4, p4, p8))
-        scan_step(3)
-        te_wait(c)
+        c_p2 = pcopy(p2, T.psa, pmm(T.psa, at, a))
+        mm(T.psz, a, x(2), True, False)
+        te.wait_ge(s_l1, 1)
+        te.wait_ge(c_p2, 1)
+        m_z = mm(T.psz, p2, l1, False, True)
+        s_z = vcopy(T.zs[:], T.psz, m_z)
+        s_l3 = vadd(l3, ps(T.psz), x(3))
 
-    if not last:
         total = 0
-        for sem, src, land, arr in ((s_x, col(T.xs, S - 1), "lx%d", "arx%d"), (s_z, T.zs[:], "land%d", "arr%d")):
-            g.wait_ge(sem, 16 if sem is s_x else 1)
+        for sem, cnt, src, land, arr in ((s_x, 16, x(S - 1), "lx%d", "arx%d"), (s_z, 1, T.zs[:], "land%d", "arr%d")):
+            g.wait_ge(sem, cnt)
             for call in plans[r]:
                 transfers = []
                 for d, engines in call:
@@ -158,52 +149,78 @@ def rank_program(g, core, T, topo):
 
     s_st0, s_st1 = ev(), ev()
     if r == 0:
+        s_l2 = vadd(l2, ps(T.psh), x(2), mm(T.psh, a, l1))
         sc.wait_ge(s_x, 16)
-        sc.dma_start(col(T.y, 0), l(0)).then_inc(s_st1, 16)
+        sc.dma_start(col(T.y, 0), x(0)).then_inc(s_st1, 16)
         sc.wait_ge(s_st1, 16)
-        for s in range(1, S):
-            sy.wait_ge(s_l[s], 1)
+        for w in (s_l1, s_l2, s_l3):
+            sy.wait_ge(w, 1)
         sy.dma_start(T.y[:, B:S * B], T.ls[:, B:S * B]).then_inc(s_st0, 16)
         sy.wait_ge(s_st0, 16)
         return
 
-    te.wait_ge(s_l[S - 1], 1)
-    for s in range(1, S):
-        ve.wait_ge(s_l[s], 1)
-    s_t, s_h = ev(), ev()
-    p = r - 1
-    ve.wait_ge(T.sem["arx%d" % p], arrives[p])
-    ve.wait_ge(T.sem["arr%d" % p], arrives[p])
-    ve.tensor_tensor((T.hs if r == 1 else T.ts)[:], T["lx%d" % p][:], T["land%d" % p][:], add).then_inc(s_h if r == 1 else s_t, 1)
-    if r > 1:
-        early = sorted(range(p), key=lambda q: topo.chip(T.cores[q]) != topo.chip(core))
-        parts = [("lx%d", "arx%d", q) for q in early] + [("land%d", "arr%d", q) for q in early]
-        m = ev()
-        for i, (land, arr, q) in enumerate(parts):
-            te.wait_ge(T.sem[arr % q], arrives[q])
-            ins = te.matmul(T.psg[:, 0:B], p4 if p - q == 1 else p8, T[land % q][:], i == 0, i == len(parts) - 1)
-        ins.then_inc(m, 1)
-        ve.wait_ge(s_t, 1)
-        ve.wait_ge(m, 1)
-        ve.tensor_tensor(T.hs[:], T.psg[:, 0:B], T.ts[:], add).then_inc(s_h, 1)
-    te.wait_ge(s_h, 1)
-    h = T.hs[:]
+    if not last:
+        te.wait_ge(pcopy(at2, T.psb, pmm(T.psb, a, at)), 1)
+        te.wait_ge(pcopy(p4, T.psc, pmm(T.psc, at2, p2)), 1)
+    else:
+        te.wait_ge(s_at, 16)
+        m0, m1 = pmm(T.psa, at, a), pmm(T.psb, a, at)
+        te.wait_ge(s_x, 16)
+        m2 = mm(T.psh, a, x(0))
+        c_p2, c_at2 = pcopy(p2, T.psa, m0), pcopy(at2, T.psb, m1)
+        s_l1 = vadd(l1, ps(T.psh), x(1), m2)
+        te.wait_ge(c_p2, 1)
+        te.wait_ge(c_at2, 1)
+        m0, m1 = pmm(T.psc, at2, p2), pmm(T.pse, p2, at2)
+        mm(T.psz, a, x(2), True, False)
+        te.wait_ge(s_l1, 1)
+        m_z = mm(T.psz, p2, l1, False, True)
+        c_p4, c_at4 = pcopy(p4, T.psc, m0), pcopy(at4, T.pse, m1)
+        s_l3 = vadd(l3, ps(T.psz), x(3), m_z)
+        te.wait_ge(c_p4, 1)
+        te.wait_ge(c_at4, 1)
+        c_p8 = pcopy(p8, T.psf, pmm(T.psf, at4, p4))
 
-    s_c = [ev(), ev()]
-    s_y = [ev(), ev()]
-    for s, bank in enumerate((T.psa, T.psb, T.psc, T.psh)):
-        m = ev()
-        if s >= 2:
-            te.wait_ge(s_c[s - 2], 1)
-        te.matmul(bank[:, 0:B], a if s == 0 else p2, h if s < 2 else col(T.cs, s - 2), True, True).then_inc(m, 1)
-        ve.wait_ge(m, 1)
-        if s < 2:
-            ve.tensor_copy(col(T.cs, s), bank[:, 0:B]).then_inc(s_c[s], 1)
-        ve.tensor_tensor(col(T.ys, s), bank[:, 0:B], l(s), add).then_inc(s_y[s // 2], 1)
+    three = ((1, T.psa, p2, l1), (0, T.psb, a, x(0)), (3, T.psc, p4, l3))
+    s_y = [None] * S
+    ve.wait_ge(s_l1, 1)
+    ve.wait_ge(s_l3, 1)
+    if r == 1:
+        landed(te, "arx%d", 0)
+        for s, bank, lhsT, own in three:
+            mm(bank, lhsT, T.lx0[:], True, False)
+        landed(te, "arr%d", 0)
+        for s, bank, lhsT, own in three:
+            s_y[s] = vadd(col(T.ys, s), ps(bank), own, mm(bank, lhsT, T.land0[:], False, True))
+    else:
+        p = r - 1
+        pw = {p - 1: p4, p - 2: p8}
+        first = True
+        for q in range(p - 1, -1, -1):
+            if pw[q] is p8:
+                te.wait_ge(c_p8, 1)
+            landed(te, "arx%d", q)
+            mm(T.psg, pw[q], T["lx%d" % q][:], first, False)
+            first = False
+        late = sorted(range(p), key=lambda q: topo.chip(T.cores[q]) != topo.chip(core))
+        for q in late:
+            landed(te, "arr%d", q)
+            m_g = mm(T.psg, pw[q], T["land%d" % q][:], False, q == late[-1])
+        landed(ve, "arx%d", p)
+        landed(ve, "arr%d", p)
+        s_t = vadd(T.ts[:], T["lx%d" % p][:], T["land%d" % p][:])
+        te.wait_ge(vadd(T.hs[:], ps(T.psg), T.ts[:], s_t, m_g), 1)
+        for s, bank, lhsT, own in three:
+            s_y[s] = vadd(col(T.ys, s), ps(bank), own, mm(bank, lhsT, T.hs[:]))
+    te.wait_ge(s_y[1], 1)
+    s_y[2] = vadd(col(T.ys, 2), ps(T.psh), x(2), mm(T.psh, a, col(T.ys, 1)))
+
     half = S * B // 2
-    sy.wait_ge(s_y[0], 2)
+    sy.wait_ge(s_y[0], 1)
+    sy.wait_ge(s_y[1], 1)
     sy.dma_start(T.y[:, 0:half], T.ys[:, 0:half]).then_inc(s_st0, 16)
-    sc.wait_ge(s_y[1], 2)
+    sc.wait_ge(s_y[2], 1)
+    sc.wait_ge(s_y[3], 1)
     sc.dma_start(T.y[:, half:2 * half], T.ys[:, half:2 * half]).then_inc(s_st1, 16)
     sy.wait_ge(s_st0, 16)
     sc.wait_ge(s_st1, 16)

from concourse.bass import DstId, RemoteDMATransfer
from concourse.mybir import AluOpType

B = 64
S = 4
N_EVENTS = 48

SCRATCH = {
    "xs": ("sbuf", [128, S * B], "float32"),
    "ls": ("sbuf", [128, S * B], "float32"),
    "ys": ("sbuf", [128, S * B], "float32"),
    "p1": ("sbuf", [128, 128], "float32"),
    "p2": ("sbuf", [128, 128], "float32"),
    "p4": ("sbuf", [128, 128], "float32"),
    "p8": ("sbuf", [128, 128], "float32"),
    "ats": ("sbuf", [128, 128], "float32"),
    "at2": ("sbuf", [128, 128], "float32"),
    "at4": ("sbuf", [128, 128], "float32"),
    "land0": ("sbuf", [128, B], "float32"),
    "land1": ("sbuf", [128, B], "float32"),
    "land2": ("sbuf", [128, B], "float32"),
    "lx0": ("sbuf", [128, B], "float32"),
    "lx1": ("sbuf", [128, B], "float32"),
    "lx2": ("sbuf", [128, B], "float32"),
    "zs": ("sbuf", [128, B], "float32"),
    "ts": ("sbuf", [128, B], "float32"),
    "hs": ("sbuf", [128, B], "float32"),
    "psh": ("psum", [128, 512], "float32"),
    "psz": ("psum", [128, 512], "float32"),
    "psa": ("psum", [128, 512], "float32"),
    "psb": ("psum", [128, 512], "float32"),
    "psc": ("psum", [128, 512], "float32"),
    "pse": ("psum", [128, 512], "float32"),
    "psf": ("psum", [128, 512], "float32"),
    "psg": ("psum", [128, 512], "float32"),
}
SEMAPHORES = ["arr0", "arr1", "arr2", "arx0", "arx1", "arx2", "sent"] + ["e%d" % i for i in range(N_EVENTS)]


def _engines(mask):
    return [i for i in range(mask.bit_length()) if (mask >> i) & 1]


def _plan(core, dests, topo):
    far = [d for d in reversed(dests) if topo.chip(d) != topo.chip(core)]
    near = [d for d in dests if topo.chip(d) == topo.chip(core)]
    far_pool = _engines(topo.mask(core, far[0])) if far else []
    calls = [[(d, far_pool)] for d in far] or [[]]
    for j, d in enumerate(near):
        pool = [e for e in _engines(topo.mask(core, d)) if e not in far_pool]
        calls[0].append((d, pool[j::len(near)]))
    return calls


def rank_program(g, core, T, topo):
    r = T.rank_of(core)
    if r is None:
        return
    n = len(T.cores)
    te, ve, sy, sc = g.tensor, g.vector, g.sync, g.scalar
    add = AluOpType.add
    used = [0]

    def ev():
        used[0] += 1
        return T.sem["e%d" % (used[0] - 1)]

    def col(t, s):
        return t[:, s * B:(s + 1) * B]

    def x(s):
        return col(T.xs, s)

    a, p2, p4, p8, at, at2, at4 = T.p1[:], T.p2[:], T.p4[:], T.p8[:], T.ats[:], T.at2[:], T.at4[:]
    l1, l2, l3 = col(T.ls, 1), col(T.ls, 2), col(T.ls, 3)
    last = r == n - 1
    plans = [_plan(c, T.cores[q + 1:], topo) for q, c in enumerate(T.cores[:-1])]
    arrives = [sum(len(e) for call in plans[q] for d, e in call if d == core) for q in range(r)]

    s_x, s_a, s_at = ev(), ev(), ev()
    sc.dma_start(a, T.a[:]).then_inc(s_a, 16)
    if last:
        sy.dma_start(at, T.at[:]).then_inc(s_at, 16)
        sy.dma_start(T.xs[:], T.x[:]).then_inc(s_x, 16)
    else:
        sy.dma_start(T.xs[:], T.x[:]).then_inc(s_x, 16)
        sc.dma_start(at, T.at[:]).then_inc(s_at, 16)

    def mm(bank, lhsT, rhs, start=True, stop=True, w=B):
        ins = te.matmul(bank[:, 0:w], lhsT, rhs, start, stop)
        if not stop:
            return None
        m = ev()
        ins.then_inc(m, 1)
        return m

    def vcopy(out, bank, m, w=B):
        ve.wait_ge(m, 1)
        c = ev()
        ve.tensor_copy(out, bank[:, 0:w]).then_inc(c, 1)
        return c

    def pmm(bank, lhsT, rhs):
        return mm(bank, lhsT, rhs, True, True, 128)

    def pcopy(out, bank, m):
        return vcopy(out, bank, m, 128)

    def vadd(out, in0, in1, *after):
        for w in after:
            ve.wait_ge(w, 1)
        c = ev()
        ve.tensor_tensor(out, in0, in1, add).then_inc(c, 1)
        return c

    def ps(bank):
        return bank[:, 0:B]

    def landed(queue, kind, q):
        queue.wait_ge(T.sem[kind % q], arrives[q])

    te.wait_ge(s_a, 16)
    ve.wait_ge(s_x, 16)
    if not last:
        te.wait_ge(s_x, 16)
        s_l1 = vadd(l1, ps(T.psh), x(1), mm(T.psh, a, x(0)))
        te.wait_ge(s_at, 16)
        c_p2 = pcopy(p2, T.psa, pmm(T.psa, at, a))
        mm(T.psz, a, x(2), True, False)
        te.wait_ge(s_l1, 1)
        te.wait_ge(c_p2, 1)
        m_z = mm(T.psz, p2, l1, False, True)
        s_z = vcopy(T.zs[:], T.psz, m_z)
        s_l3 = vadd(l3, ps(T.psz), x(3))

        total = 0
        for sem, cnt, src, land, arr in ((s_x, 16, x(S - 1), "lx%d", "arx%d"), (s_z, 1, T.zs[:], "land%d", "arr%d")):
            g.wait_ge(sem, cnt)
            for call in plans[r]:
                transfers = []
                for d, engines in call:
                    rid, pid, _ = topo.addr(d)
                    transfers.append(RemoteDMATransfer(dst_ids=[DstId(rid=rid, pnc=pid)],
                                                       dma_engine_mask=sum(1 << e for e in engines),
                                                       remote_sem=T.sem[arr % r], src=src, dst=T[land % r][:]))
                    total += len(engines)
                g.remote_dma_fused(transfers, local_sem=T.sem.sent)
        g.wait_ge(T.sem.sent, total)

    s_st0, s_st1 = ev(), ev()
    if r == 0:
        s_l2 = vadd(l2, ps(T.psh), x(2), mm(T.psh, a, l1))
        sc.wait_ge(s_x, 16)
        sc.dma_start(col(T.y, 0), x(0)).then_inc(s_st1, 16)
        sc.wait_ge(s_st1, 16)
        for w in (s_l1, s_l2, s_l3):
            sy.wait_ge(w, 1)
        sy.dma_start(T.y[:, B:S * B], T.ls[:, B:S * B]).then_inc(s_st0, 16)
        sy.wait_ge(s_st0, 16)
        return

    if not last:
        te.wait_ge(pcopy(at2, T.psb, pmm(T.psb, a, at)), 1)
        te.wait_ge(pcopy(p4, T.psc, pmm(T.psc, at2, p2)), 1)
    else:
        te.wait_ge(s_at, 16)
        m0, m1 = pmm(T.psa, at, a), pmm(T.psb, a, at)
        te.wait_ge(s_x, 16)
        m2 = mm(T.psh, a, x(0))
        c_p2, c_at2 = pcopy(p2, T.psa, m0), pcopy(at2, T.psb, m1)
        s_l1 = vadd(l1, ps(T.psh), x(1), m2)
        te.wait_ge(c_p2, 1)
        te.wait_ge(c_at2, 1)
        m0, m1 = pmm(T.psc, at2, p2), pmm(T.pse, p2, at2)
        mm(T.psz, a, x(2), True, False)
        te.wait_ge(s_l1, 1)
        m_z = mm(T.psz, p2, l1, False, True)
        c_p4, c_at4 = pcopy(p4, T.psc, m0), pcopy(at4, T.pse, m1)
        s_l3 = vadd(l3, ps(T.psz), x(3), m_z)
        te.wait_ge(c_p4, 1)
        te.wait_ge(c_at4, 1)
        c_p8 = pcopy(p8, T.psf, pmm(T.psf, at4, p4))

    three = ((1, T.psa, p2, l1), (0, T.psb, a, x(0)), (3, T.psc, p4, l3))
    s_y = [None] * S
    ve.wait_ge(s_l1, 1)
    ve.wait_ge(s_l3, 1)
    if r == 1:
        landed(te, "arx%d", 0)
        for s, bank, lhsT, own in three:
            mm(bank, lhsT, T.lx0[:], True, False)
        landed(te, "arr%d", 0)
        for s, bank, lhsT, own in three:
            s_y[s] = vadd(col(T.ys, s), ps(bank), own, mm(bank, lhsT, T.land0[:], False, True))
    else:
        p = r - 1
        pw = {p - 1: p4, p - 2: p8}
        first = True
        for q in range(p - 1, -1, -1):
            if pw[q] is p8:
                te.wait_ge(c_p8, 1)
            landed(te, "arx%d", q)
            mm(T.psg, pw[q], T["lx%d" % q][:], first, False)
            first = False
        late = sorted(range(p), key=lambda q: topo.chip(T.cores[q]) != topo.chip(core))
        for q in late:
            landed(te, "arr%d", q)
            m_g = mm(T.psg, pw[q], T["land%d" % q][:], False, q == late[-1])
        landed(ve, "arx%d", p)
        landed(ve, "arr%d", p)
        s_t = vadd(T.ts[:], T["lx%d" % p][:], T["land%d" % p][:])
        te.wait_ge(vadd(T.hs[:], ps(T.psg), T.ts[:], s_t, m_g), 1)
        for s, bank, lhsT, own in three:
            s_y[s] = vadd(col(T.ys, s), ps(bank), own, mm(bank, lhsT, T.hs[:]))
    te.wait_ge(s_y[1], 1)
    s_y[2] = vadd(col(T.ys, 2), ps(T.psh), x(2), mm(T.psh, a, col(T.ys, 1)))

    half = S * B // 2
    sy.wait_ge(s_y[0], 1)
    sy.wait_ge(s_y[1], 1)
    sy.dma_start(T.y[:, 0:half], T.ys[:, 0:half]).then_inc(s_st0, 16)
    sc.wait_ge(s_y[2], 1)
    sc.wait_ge(s_y[3], 1)
    sc.dma_start(T.y[:, half:2 * half], T.ys[:, half:2 * half]).then_inc(s_st1, 16)
    sy.wait_ge(s_st0, 16)
    sc.wait_ge(s_st1, 16)
